import numpy as np
import ml_dtypes


def mxq(x, axis, fmt="e4m3"):
    dtype, down = {"e4m3": (ml_dtypes.float8_e4m3fn, 7), "e5m2": (ml_dtypes.float8_e5m2, 14)}[fmt]
    v = np.moveaxis(np.asarray(x, np.float32).astype(ml_dtypes.bfloat16).astype(np.float64), axis, -1)
    blocks = v.reshape(v.shape[:-1] + (-1, 32))
    amax = np.abs(blocks).max(-1, keepdims=True)
    byte = np.maximum(np.where(amax > 0, np.frexp(amax)[1] - 1 + 127, 0) - down, 1)
    scale = np.exp2(byte - 127.0)
    codes = (blocks / scale).astype(np.float32).astype(dtype).astype(np.float64)
    return np.moveaxis((codes * scale).reshape(v.shape), -1, axis)


WIDE = False


def mx_kscale(k):
    if not WIDE:
        return np.ones(k)
    levels = np.array([10, -10, 5, -5, 0])
    if k % 512:
        return np.exp2(np.random.permutation(np.resize(levels, k // 32))).repeat(32)
    a = np.empty((k // 512, 16))
    for p in range(k // 512):
        a[p, :8] = np.random.permutation(np.resize(levels, 8))
        for g in range(8):
            far = levels[np.abs(levels - a[p, g]) >= 10]
            a[p, g + 8] = far[np.random.randint(len(far))]
    return np.exp2(a.ravel()).repeat(32)


BF16 = ml_dtypes.bfloat16


def bf(x):
    return np.asarray(x, np.float32).astype(BF16)


def f64(x):
    return np.asarray(x).astype(np.float64)


E2M1 = np.array([0.0, 0.5, 1.0, 1.5, 2.0, 3.0, 4.0, 6.0, -0.0, -0.5, -1.0, -1.5, -2.0, -3.0, -4.0, -6.0])


def pack_weight(w, fmt):
    k, n = w.shape
    w = f64(bf(w)).reshape(k // 32, 32, n)
    amax = np.abs(w).max(1)
    if fmt == "e4m3":
        byte = np.frexp(amax)[1] - 1 + 127 - 7
    else:
        mant, ex = np.frexp(amax / 6.0)
        byte = np.where(mant > 0.5, ex, ex - 1) + 127
    byte = np.clip(np.where(amax > 0, byte, 1), 1, 254)
    scaled = (w * np.exp2(127.0 - byte)[:, None, :]).reshape(k, n).astype(np.float32)
    by_word = np.ascontiguousarray(scaled.reshape(k // 512, 128, 4, n).transpose(0, 1, 3, 2))
    if fmt == "e4m3":
        words = by_word.astype(ml_dtypes.float8_e4m3fn).view(np.uint8)
    else:
        c = by_word.astype(ml_dtypes.float4_e2m1fn).view(np.uint8) & 0xF
        words = c[..., 0::2] | (c[..., 1::2] << 4)
    return np.ascontiguousarray(words), np.ascontiguousarray(byte.astype(np.uint8).reshape(k // 512, 16, n))


def unpack_weight(words, scales, fmt):
    g, p, n, _ = words.shape
    if fmt == "e4m3":
        vals = np.ascontiguousarray(words).view(ml_dtypes.float8_e4m3fn).astype(np.float64)
    else:
        nib = np.empty((g, p, n, 4), np.uint8)
        nib[..., 0::2] = words & 0xF
        nib[..., 1::2] = words >> 4
        vals = E2M1[nib]
    vals = vals * np.repeat(np.exp2(scales.astype(np.float64) - 127.0), 8, axis=1)[..., None]
    return vals.transpose(0, 1, 3, 2).reshape(g * 512, n)
def pack4(w):
    words, scales = pack_weight(w, "e2m1")
    return words.reshape(words.shape[0], 128, -1), scales


def unpack4(words, scales):
    return unpack_weight(words.reshape(words.shape[0], 128, -1, 2), scales, "e2m1")


def planes(Y):
    n, m = Y.shape
    b = f64(bf(Y)).reshape(n // 32, 32, m)
    amax = np.abs(b).max(1)
    byte = np.clip(np.where(amax > 0, np.frexp(amax)[1] - 1 + 127 - 7, 1), 1, 254)
    codes = (b * np.exp2(127.0 - byte)[:, None, :]).reshape(n, m).astype(np.float32).astype(ml_dtypes.float8_e4m3fn).view(np.uint8)
    words = codes.reshape(n // 512, 128, 4, m).transpose(0, 1, 3, 2)
    return np.ascontiguousarray(words), np.ascontiguousarray(byte.astype(np.uint8).reshape(n // 512, 16, m))


N, J, D, T = 2048, 512, 1024, 1024


def outcome_residual(y, xq, etaq):
    return y - (xq @ etaq)


def signed_weights(l):
    p = np.exp(l)
    q = np.exp(-l)
    s = np.sum((p + q) / 2.0, axis=1)
    return ((p - q) / 2.0) / s[:, None]


def setup_inputs():
    s, t = mx_kscale(D), mx_kscale(J)
    c = np.sqrt(J) / 8.0
    y1 = bf(np.random.standard_normal((N, T)))
    x1 = bf(np.random.standard_normal((N, D)) * s[None, :])
    y0 = bf(np.random.standard_normal((J, T)) * c / t[:, None])
    x0 = bf(np.random.standard_normal((J, D)) * c * s[None, :] / t[:, None])
    words, scales = pack4(np.random.standard_normal((D, T)) / np.sqrt(D) / s[:, None])
    return {
        "y1": y1,
        "x1": x1,
        "y0": y0,
        "x0": x0,
        "eta_words": words,
        "eta_scales": scales,
        "l": bf(np.random.standard_normal((N, J)) * 2.0),
        "a": bf(np.random.uniform(0.5, 1.5, J) * t),
    }


def core(y1, x1, y0, x0, eta_words, eta_scales, l, a):
    etaq = unpack4(eta_words, eta_scales)
    e1 = outcome_residual(f64(y1), mxq(f64(x1), 1, "e4m3"), etaq)
    e0 = outcome_residual(f64(y0), mxq(f64(x0), 1, "e4m3"), etaq)
    w = signed_weights(f64(l))
    wa = w * f64(a)[None, :]
    gap = e1 - (mxq(wa, 1, "e4m3") @ mxq(e0, 0, "e4m3"))
    return gap


def reference(y1, x1, y0, x0, eta_words, eta_scales, l, a):
    R_out = core(y1, x1, y0, x0, eta_words, eta_scales, l, a)
    words, scales = planes(R_out.T)
    return R_out, words, scales

@@ -1,0 +1,418 @@
+from contextlib import ExitStack
+
+import concourse.mybir as mybir
+from concourse.masks import make_identity
+
+N, J, D, T = 2048, 512, 1024, 1024
+FLOPS = 2 * N * D * T + 2 * J * D * T + 2 * N * J * T
+
+F32 = mybir.dt.float32
+BF16 = mybir.dt.bfloat16
+I32 = mybir.dt.int32
+U32 = mybir.dt.uint32
+U8 = mybir.dt.uint8
+FP8X4 = mybir.dt.float8_e4m3fn_x4
+FP4X4 = mybir.dt.float4_e2m1fn_x4
+ALU = mybir.AluOpType
+ACT = mybir.ActivationFunctionType
+AX = mybir.AxisListType
+
+P = 128
+TILES = N // P
+PAIRS = TILES // 2
+
+LOAD_GROUPS = {'l': [(0, 1), (1, 2), (2, 4), (4, 8)], 'x': [(0, 1), (1, 2), (2, 4), (4, 6), (6, 8)], 'y': [(0, 1), (1, 2), (2, 4), (4, 6), (6, 8)]}
+BUFS = {'tp': 4, 'acc': 3, 'pq': 3, 'd': 2, 'w': 2, 'xg': 3, 'wg': 3, 'o': 6, 'ob': 6, 'og': 3, 'xc': 3, 'xs': 3, 'wc': 3, 'ws': 3}
+ON_VECTOR = {'CX0': [0], 'CX': [], 'CW': [12], 'CO': [13], 'CAST': [(14, 0), (15, 0)]}
+ON_GPSIMD = {'DIF': [1, 2, 3, 4, 5, 6, 7, 8, 9, 10, 11, 12, 13, 14, 15], 'CAST': [(1, 0), (0, 1), (2, 0), (3, 0), (4, 0), (5, 0), (6, 0), (6, 1), (8, 0), (10, 0), (11, 0), (12, 1), (13, 1), (15, 1)]}
+ORDER = [
+    ('GA',), ('MS',), ('GW',), ('GO',), ('LOAD', 'l', 0), ('LX0', 0), ('LX0', 2), ('LOAD', 'l', 1),
+    ('LX0', 3), ('LA',), ('LOAD', 'l', 2), ('LX0', 1), ('LOAD', 'x', 0), ('LES',), ('LEW',), ('LY0', 0),
+    ('W', 0), ('GI',), ('W', 1), ('LOAD', 'x', 1), ('LY0', 1), ('W', 2), ('TX0', 0), ('W', 3),
+    ('MAX', 0), ('TX0', 2), ('MAX', 1), ('W', 4), ('W', 5), ('W', 6), ('TX0', 3), ('NEG', 0),
+    ('TX0', 1), ('LOAD', 'x', 2), ('MAX', 2), ('EXP', 0), ('NEG', 1), ('W', 7), ('SUM', 0), ('MAX', 3),
+    ('REC', 0), ('MA',), ('EXP', 1), ('NEG', 2), ('DIF', 0), ('CX0', 0), ('CX0', 3), ('SUM', 1),
+    ('MAX', 4), ('CX0', 2), ('REC', 1), ('TX', 1), ('EXP', 2), ('LOAD', 'l', 3), ('LOAD', 'y', 0), ('NEG', 3),
+    ('CX0', 1), ('DIF', 1), ('SUM', 2), ('MAX', 5), ('QX0', 1), ('STT', 0), ('QX0', 0), ('CX', 1),
+    ('REC', 2), ('TX', 0), ('TW', 0), ('STT', 1), ('EXP', 3), ('NEG', 4), ('CW', 0), ('ME', 3),
+    ('ME', 0), ('DIF', 2), ('SUM', 3), ('MAX', 6), ('QW', 0), ('REC', 3), ('TW', 1), ('ME', 1),
+    ('SE', 3), ('SE', 0), ('ME', 2), ('STT', 2), ('QX', 1), ('EXP', 4), ('NEG', 5), ('ME', 4),
+    ('CW', 1), ('LOAD', 'y', 2), ('LOAD', 'y', 1), ('CX', 0), ('QW', 1), ('LOAD', 'x', 3), ('SE', 1), ('SE', 2),
+    ('TX', 2), ('SE', 4), ('ME', 7), ('ME', 5), ('DIF', 3), ('QE', 0), ('SE', 7), ('QX', 0),
+    ('CX', 2), ('ME', 6), ('TX', 3), ('SE', 5), ('SUM', 4), ('MAX', 7), ('SE', 6), ('CX', 3),
+    ('REC', 4), ('QE', 1), ('TW', 2), ('TX', 4), ('STT', 3), ('QX', 2), ('MX', 0, 0), ('EXP', 5),
+    ('NEG', 6), ('CW', 2), ('MX', 1, 0), ('MX', 1, 1), ('QW', 2), ('SUB', 0, 0), ('DIF', 4), ('SUB', 1, 0),
+    ('SUM', 5), ('MAX', 8), ('CX', 4), ('REC', 5), ('SUB', 1, 1), ('TW', 3), ('TX', 5), ('STT', 4),
+    ('MX', 0, 1), ('QX', 3), ('EXP', 6), ('NEG', 7), ('CW', 3), ('MX', 2, 0), ('MX', 2, 1), ('QW', 3),
+    ('DIF', 5), ('SUB', 0, 1), ('SUB', 2, 0), ('SUM', 6), ('MAX', 9), ('CAST', 1, 0), ('CAST', 0, 0), ('CX', 5),
+    ('REC', 6), ('SUB', 2, 1), ('TW', 4), ('TO', 0), ('TX', 6), ('STT', 5), ('QX', 4), ('EXP', 7),
+    ('NEG', 8), ('CW', 4), ('MX', 3, 0), ('MX', 3, 1), ('QW', 4), ('DIF', 6), ('CAST', 0, 1), ('CAST', 1, 1),
+    ('SUB', 3, 0), ('SUM', 7), ('MAX', 10), ('CAST', 2, 0), ('CX', 6), ('REC', 7), ('SUB', 3, 1), ('TW', 5),
+    ('TX', 7), ('STT', 6), ('QX', 5), ('EXP', 8), ('NEG', 9), ('CW', 5), ('MX', 4, 0), ('MX', 4, 1),
+    ('QW', 5), ('DIF', 7), ('CO', 0), ('CAST', 2, 1), ('TO', 1), ('SUB', 4, 0), ('SUM', 8), ('MAX', 11),
+    ('CAST', 3, 0), ('CX', 7), ('REC', 8), ('SUB', 4, 1), ('TW', 6), ('TX', 8), ('STT', 7), ('QO', 0),
+    ('QX', 6), ('EXP', 9), ('NEG', 10), ('CW', 6), ('MX', 5, 0), ('MX', 5, 1), ('QW', 6), ('STO', 0),
+    ('DIF', 8), ('CO', 1), ('CAST', 3, 1), ('SUB', 5, 0), ('SUM', 9), ('MAX', 12), ('CAST', 4, 0), ('CX', 8),
+    ('REC', 9), ('SUB', 5, 1), ('TW', 7), ('TO', 2), ('TX', 9), ('STT', 8), ('QO', 1), ('QX', 7),
+    ('EXP', 10), ('NEG', 11), ('CW', 7), ('MX', 6, 0), ('MX', 6, 1), ('LOAD', 'x', 4), ('QW', 7), ('STO', 1),
+    ('DIF', 9), ('CO', 2), ('CAST', 4, 1), ('SUB', 6, 0), ('SUM', 10), ('MAX', 13), ('CAST', 5, 0), ('CX', 9),
+    ('REC', 10), ('SUB', 6, 1), ('TW', 8), ('TO', 3), ('TX', 10), ('STT', 9), ('QO', 2), ('QX', 8),
+    ('EXP', 11), ('NEG', 12), ('CW', 8), ('MX', 7, 0), ('MX', 7, 1), ('QW', 8), ('TX', 12), ('DIF', 10),
+    ('CO', 3), ('CAST', 5, 1), ('SUB', 7, 0), ('SUM', 11), ('MAX', 14), ('CAST', 6, 0), ('CX', 10), ('REC', 11),
+    ('SUB', 7, 1), ('TW', 9), ('TO', 4), ('TX', 11), ('STT', 10), ('QO', 3), ('QX', 9), ('LOAD', 'y', 3),
+    ('EXP', 12), ('NEG', 13), ('CW', 9), ('MX', 8, 0), ('MX', 8, 1), ('QW', 9), ('STO', 3), ('STO', 2),
+    ('DIF', 11), ('CO', 4), ('CAST', 6, 1), ('SUB', 8, 0), ('SUM', 12), ('MAX', 15), ('CX', 12), ('CAST', 7, 0),
+    ('CX', 11), ('REC', 12), ('SUB', 8, 1), ('TW', 10), ('TO', 5), ('STT', 11), ('QO', 4), ('QX', 10),
+    ('EXP', 13), ('NEG', 14), ('TX', 13), ('CW', 10), ('MX', 9, 0), ('MX', 9, 1), ('QW', 10), ('STO', 4),
+    ('DIF', 12), ('CO', 5), ('CAST', 7, 1), ('SUB', 9, 0), ('CAST', 8, 0), ('SUM', 13), ('REC', 13), ('SUB', 9, 1),
+    ('TW', 11), ('TO', 6), ('STT', 12), ('QO', 5), ('QX', 11), ('CX', 13), ('EXP', 14), ('NEG', 15),
+    ('CW', 11), ('MX', 10, 0), ('MX', 10, 1), ('QW', 11), ('STO', 5), ('DIF', 13), ('CO', 6), ('CAST', 8, 1),
+    ('SUB', 10, 0), ('SUM', 14), ('CAST', 9, 0), ('REC', 14), ('SUB', 10, 1), ('TW', 12), ('CW', 12), ('TO', 7),
+    ('TX', 14), ('QO', 6), ('QX', 12), ('EXP', 15), ('LOAD', 'y', 4), ('MX', 11, 0), ('MX', 11, 1), ('QW', 12),
+    ('STO', 6), ('DIF', 14), ('STT', 13), ('CO', 7), ('MX', 12, 0), ('CAST', 9, 1), ('SUB', 11, 0), ('SUM', 15),
+    ('CAST', 10, 0), ('CX', 14), ('REC', 15), ('STT', 14), ('SUB', 11, 1), ('TW', 13), ('TO', 8), ('TX', 15),
+    ('QO', 7), ('QX', 13), ('CW', 13), ('QW', 13), ('STO', 7), ('DIF', 15), ('CO', 8), ('CAST', 10, 1),
+    ('SUB', 12, 0), ('CAST', 11, 0), ('CX', 15), ('TW', 14), ('TO', 9), ('STT', 15), ('QO', 8), ('MX', 12, 1),
+    ('QX', 14), ('CW', 14), ('MX', 13, 0), ('MX', 13, 1), ('QW', 14), ('SUB', 12, 1), ('STO', 8), ('CO', 9),
+    ('CAST', 11, 1), ('SUB', 13, 0), ('CAST', 12, 0), ('SUB', 13, 1), ('TW', 15), ('TO', 10), ('QO', 9), ('QX', 15),
+    ('STW', 0, 2), ('CW', 15), ('MX', 14, 0), ('MX', 14, 1), ('QW', 15), ('STO', 9), ('CO', 10), ('CAST', 12, 1),
+    ('SUB', 14, 0), ('CAST', 13, 0), ('SUB', 14, 1), ('TO', 11), ('QO', 10), ('CAST', 14, 0), ('MX', 15, 0), ('MX', 15, 1),
+    ('STO', 10), ('CO', 11), ('CAST', 13, 1), ('TO', 12), ('QO', 11), ('STW', 2, 4), ('STO', 11), ('SUB', 15, 0),
+    ('CO', 12), ('CAST', 14, 1), ('SUB', 15, 1), ('CAST', 15, 0), ('TO', 13), ('QO', 12), ('STO', 12), ('CO', 13),
+    ('CAST', 15, 1), ('TO', 14), ('QO', 13), ('STO', 13), ('CO', 14), ('TO', 15), ('QO', 14), ('STO', 14),
+    ('CO', 15), ('STS', 0, 6), ('STW', 4, 6), ('QO', 15), ('STO', 15), ('STW', 6, 7), ('STS', 6, 8), ('STW', 7, 8),
+]
+
+
+def group_of(kind, pair):
+    return [j for j, (lo, hi) in enumerate(LOAD_GROUPS[kind]) if lo <= pair < hi][0]
+
+
+def tile_augmentedl1ballsyntheticcontrolgap_x2_kernel(
+    tc, y1, x1, y0, x0, eta_words, eta_scales, l, a, out_0, out_1, out_2
+):
+    nc = tc.nc
+    with ExitStack() as ctx:
+        keep = ctx.enter_context(tc.tile_pool(name="keep", bufs=1))
+        work = ctx.enter_context(tc.tile_pool(name="work", bufs=2))
+        stat = ctx.enter_context(tc.tile_pool(name="stat", bufs=TILES))
+        psum = ctx.enter_context(tc.psum_pool(name="psum", bufs=1))
+        ctx.enter_context(tc.manual_schedule())
+
+        ident = keep.tile([P, P], F32, name="ident")
+        ones = keep.tile([P, P], BF16, name="ones")
+        a_row = keep.tile([P, J], BF16, name="a_row")
+        gain = psum.tile([P, J], F32, name="gain")
+        idle = keep.tile([P, J], BF16, name="idle")
+        eta_w = keep.tile([P, 2, 2 * T], U8, name="eta_w", align_bytes=64)
+        eta_s = keep.tile([P, 2, T], U8, name="eta_s", align_bytes=64)
+        x0_sb = keep.tile([P, 4, D], BF16, name="x0_sb")
+        y0_sb = keep.tile([P, 2, 4, 512], BF16, name="y0_sb")
+        x0_g = keep.tile([P, 4, D], BF16, name="x0_g", align_bytes=64)
+        x0_c = keep.tile([P, 4, 2, P], U32, name="x0_c", align_bytes=64)
+        x0_s = keep.tile([P, 4, 2, P], U8, name="x0_s", align_bytes=64)
+        e0_g = keep.tile([P, T, 4], BF16, name="e0_g", align_bytes=64)
+        e0_c = keep.tile([P, T], U32, name="e0_c", align_bytes=64)
+        e0_s = keep.tile([P, T], U8, name="e0_s", align_bytes=64)
+        out_c = keep.tile([P, 2, N], U32, name="out_c", align_bytes=64)
+        out_s = keep.tile([P, 2, N], U8, name="out_s", align_bytes=64)
+
+        sources = {
+            "l": l.rearrange("(s p i) k -> p s (i k)", p=P, i=2),
+            "x": x1.rearrange("(s p i) k -> p s (i k)", p=P, i=2),
+            "y": y1.rearrange("(s p i) k -> p s (i k)", p=P, i=2),
+        }
+        out_rows = out_0.rearrange("(s p i) k -> s i p k", p=P, i=2)
+        out_words = out_1.rearrange("g p m t -> p g (m t)")
+        held = {}
+
+        def bank(tag, key):
+            held[key] = psum.tile([P, 512], F32, name=tag, bufs=BUFS[tag])
+            return held[key]
+
+        def fresh(tag, n, shape, dtype):
+            held[tag, n] = work.tile(shape, dtype, name=tag, bufs=BUFS[tag], align_bytes=64)
+            return held[tag, n]
+
+        def column(tag, n, width=1):
+            held[tag, n] = stat.tile([P, width], F32, name=tag)
+            return held[tag, n]
+
+        def rows(kind, n):
+            j = group_of(kind, n // 2)
+            width = sources[kind].shape[2] // 2
+            return held[kind, j][:, n // 2 - LOAD_GROUPS[kind][j][0], (n % 2) * width : (n % 2 + 1) * width]
+
+        def load(kind, j):
+            lo, hi = LOAD_GROUPS[kind][j]
+            held[kind, j] = keep.tile([P, hi - lo, sources[kind].shape[2]], BF16, name="%s_in%d" % (kind, j))
+            nc.sync.dma_start(out=held[kind, j][:], in_=sources[kind][:, lo:hi, :])
+
+        def copy(on_vector, out, in_):
+            if on_vector:
+                nc.vector.tensor_copy(out=out, in_=in_)
+            else:
+                nc.scalar.copy(out=out, in_=in_)
+
+        def transpose_k_last(src, dst):
+            words = src.bitcast(F32)
+            for g in range(2):
+                for u in range(2):
+                    c = (2 * g + u) * P
+                    nc.tensor.transpose(dst[:, c : c + P], words[:, 256 * g + u : 256 * (g + 1) : 2], ident[:])
+
+        def gather_k_last(on_vector, src, dst):
+            copy(
+                on_vector,
+                dst.bitcast(F32).rearrange("p (g r u) -> p g r u", g=2, u=2),
+                src[:].rearrange("p (g u r) -> p g r u", g=2, u=2),
+            )
+
+        def MS():
+            nc.vector.memset(eta_s[:].rearrange("p g n -> p (g n)").bitcast(I32), 0)
+
+        def GI():
+            make_identity(nc, ident[:])
+
+        def GA():
+            nc.vector.memset(a_row[:], 0.0)
+
+        def GO():
+            nc.vector.memset(ones[:], 1.0)
+
+        def GW():
+            nc.vector.memset(idle[:], 0.0)
+
+        def W(j):
+            nc.tensor.matmul(gain[:], lhsT=ones[:], rhs=idle[:], start=True, stop=True)
+
+        def LX0(t):
+            nc.sync.dma_start(out=x0_sb[:, t, :], in_=x0.rearrange("(p t) k -> p t k", t=4)[:, t, :])
+
+        def LY0(h):
+            cols = slice(512 * h, 512 * (h + 1))
+            nc.sync.dma_start(out=y0_sb[:, h], in_=y0.rearrange("(p t) k -> p t k", t=4)[:, :, cols])
+
+        def LEW():
+            nc.sync.dma_start(out=eta_w[:].bitcast(I32), in_=eta_words.rearrange("g p b -> p g b").bitcast(I32))
+
+        def LES():
+            for q in range(4):
+                nc.sync.dma_start(
+                    out=eta_s[32 * q : 32 * q + 4, :, :].bitcast(I32),
+                    in_=eta_scales[:, 4 * q : 4 * q + 4, :].rearrange("g r n -> r g n").bitcast(I32),
+                )
+
+        def LA():
+            nc.sync.dma_start(out=a_row[0:1, :], in_=a.rearrange("(o n) -> o n", o=1))
+
+        def MA():
+            nc.tensor.matmul(
+                gain[:], lhsT=ones[:], rhs=a_row[:].rearrange("p (q u e) -> p u q e", u=2, e=2), start=True, stop=True
+            )
+
+        def TX0(t):
+            transpose_k_last(x0_sb[:, t, :], bank("tp", ("x0", t)))
+
+        def CX0(t):
+            gather_k_last(t in ON_VECTOR["CX0"], held["x0", t], x0_g[:, t, :])
+
+        def QX0(h):
+            nc.vector.quantize_mx(
+                out=x0_c[:, 2 * h : 2 * h + 2].rearrange("p t g r -> p (t g r)").bitcast(FP8X4),
+                scales=x0_s[:, 2 * h : 2 * h + 2].rearrange("p t g r -> p (t g r)"),
+                in_=x0_g[:, 2 * h : 2 * h + 2, :].rearrange("p t k -> p (t k)"),
+            )
+
+        def ME(c):
+            acc = bank("acc", ("e", c))
+            for t in range(4):
+                for g in range(2):
+                    nc.tensor.matmul_mx(
+                        out=acc[:, t * P : (t + 1) * P],
+                        lhsT=x0_c[:, t, g, :].bitcast(FP8X4),
+                        lhsT_scale=x0_s[:, t, g, :],
+                        rhs=eta_w[:, g, 2 * P * c : 2 * P * (c + 1)].bitcast(FP4X4),
+                        rhs_scale=eta_s[:, g, P * c : P * (c + 1)],
+                        start=(g == 0),
+                        stop=(g == 1),
+                    )
+
+        def SE(c):
+            nc.vector.tensor_tensor(
+                out=e0_g[:, P * c : P * (c + 1), :],
+                in0=y0_sb[:, c // 4, :, P * (c % 4) : P * (c % 4 + 1)].rearrange("p t n -> p n t"),
+                in1=held["e", c][:].rearrange("p (t n) -> p n t", t=4),
+                op=ALU.subtract,
+            )
+
+        def QE(h):
+            cols = slice(512 * h, 512 * (h + 1))
+            nc.vector.quantize_mx(
+                out=e0_c[:, cols].bitcast(FP8X4),
+                scales=e0_s[:, cols],
+                in_=e0_g[:, cols, :].rearrange("p n t -> p (n t)"),
+            )
+
+        def MAX(n):
+            nc.vector.tensor_reduce(
+                out=column("top", n)[:], in_=rows("l", n), axis=AX.X, op=ALU.max, apply_absolute_value=True
+            )
+
+        def NEG(n):
+            nc.gpsimd.tensor_scalar(
+                out=column("shift", n)[:], in0=held["top", n][:], scalar1=-1.0, scalar2=0.0, op0=ALU.mult, op1=ALU.add
+            )
+
+        def EXP(n):
+            pq = fresh("pq", n, [P, 2, J], F32)
+            sums = column("sums", n, 2)
+            for side, sign in enumerate((1.0, -1.0)):
+                nc.scalar.activation(
+                    out=pq[:, side, :].rearrange("p (u q e) -> p u q e", u=2, e=2),
+                    in_=rows("l", n).rearrange("p (q u e) -> p u q e", u=2, e=2),
+                    func=ACT.Exp,
+                    bias=held["shift", n][:],
+                    scale=sign,
+                    accum_out=sums[:, side : side + 1],
+                )
+
+        def SUM(n):
+            sums = held["sums", n]
+            nc.gpsimd.tensor_tensor(out=column("total", n)[:], in0=sums[:, 0:1], in1=sums[:, 1:2], op=ALU.add)
+
+        def REC(n):
+            nc.vector.reciprocal(out=column("recip", n)[:], in_=held["total", n][:])
+
+        def DIF(n):
+            engine = nc.gpsimd if n in ON_GPSIMD["DIF"] else nc.vector
+            pq = held["pq", n]
+            engine.tensor_tensor(out=fresh("d", n, [P, J], F32)[:], in0=pq[:, 0, :], in1=pq[:, 1, :], op=ALU.subtract)
+
+        def STT(n):
+            nc.vector.scalar_tensor_tensor(
+                out=fresh("w", n, [P, J], BF16)[:],
+                in0=held["d", n][:],
+                scalar=held["recip", n][:],
+                in1=gain[:],
+                op0=ALU.mult,
+                op1=ALU.mult,
+            )
+
+        def TX(n):
+            transpose_k_last(rows("x", n), bank("tp", ("xt", n)))
+
+        def CX(n):
+            gather_k_last(n in ON_VECTOR["CX"], held["xt", n], fresh("xg", n, [P, D], BF16)[:])
+
+        def QX(n):
+            nc.vector.quantize_mx(
+                out=fresh("xc", n, [P, 2 * P], U32)[:].bitcast(FP8X4),
+                scales=fresh("xs", n, [P, 2 * P], U8)[:],
+                in_=held["xg", n][:],
+            )
+
+        def TW(n):
+            dst = bank("tp", ("wt", n))
+            words = held["w", n][:].bitcast(F32)
+            for u in range(2):
+                nc.tensor.transpose(dst[:, u * P : (u + 1) * P], words[:, u * P : (u + 1) * P], ident[:])
+
+        def CW(n):
+            copy(
+                n in ON_VECTOR["CW"],
+                fresh("wg", n, [P, J], BF16)[:].bitcast(F32).rearrange("p (r u) -> p r u", u=2),
+                held["wt", n][:, 0 : 2 * P].rearrange("p (u r) -> p r u", u=2),
+            )
+
+        def QW(n):
+            nc.vector.quantize_mx(
+                out=fresh("wc", n, [P, P], U32)[:].bitcast(FP8X4),
+                scales=fresh("ws", n, [P, P], U8)[:],
+                in_=held["wg", n][:],
+            )
+
+        def MX(n, h):
+            acc = bank("acc", ("acc", n, h))
+            for g in range(2):
+                nc.tensor.matmul_mx(
+                    out=acc[:],
+                    lhsT=held["xc", n][:, g * P : (g + 1) * P].bitcast(FP8X4),
+                    lhsT_scale=held["xs", n][:, g * P : (g + 1) * P],
+                    rhs=eta_w[:, g, 1024 * h : 1024 * (h + 1)].bitcast(FP4X4),
+                    rhs_scale=eta_s[:, g, 512 * h : 512 * (h + 1)],
+                    start=(g == 0),
+                    stop=False,
+                )
+            nc.tensor.matmul_mx(
+                out=acc[:],
+                lhsT=held["wc", n][:].bitcast(FP8X4),
+                lhsT_scale=held["ws", n][:],
+                rhs=e0_c[:, 512 * h : 512 * (h + 1)].bitcast(FP8X4),
+                rhs_scale=e0_s[:, 512 * h : 512 * (h + 1)],
+                start=False,
+                stop=True,
+            )
+
+        def SUB(n, h):
+            o = held["o", n] if h else fresh("o", n, [P, T], F32)
+            cols = slice(512 * h, 512 * (h + 1))
+            nc.vector.tensor_tensor(
+                out=o[:, cols], in0=rows("y", n)[:, cols], in1=held["acc", n, h][:], op=ALU.subtract
+            )
+
+        def CAST(n, h):
+            dst = fresh("ob", (n, h), [P, 512], BF16)[:].rearrange("p (u q e) -> p u q e", u=2, e=2)
+            src = held["o", n][:, 512 * h : 512 * (h + 1)].rearrange("p (q u e) -> p u q e", u=2, e=2)
+            if (n, h) in ON_GPSIMD["CAST"]:
+                nc.gpsimd.tensor_scalar(out=dst, in0=src, scalar1=1.0, scalar2=1.0, op0=ALU.mult, op1=ALU.mult)
+            else:
+                copy((n, h) in ON_VECTOR["CAST"], dst, src)
+
+        def STO(n):
+            nc.sync.dma_start(out=out_rows[n // 2, n % 2], in_=held["o", n][:])
+
+        def TO(n):
+            s, g = divmod(n, 2)
+            dst = bank("tp", ("ot", n))
+            for i in range(2):
+                words = held["ob", (2 * s + i, g)][:].bitcast(F32)
+                for u in range(2):
+                    c = (2 * i + u) * P
+                    nc.tensor.transpose(dst[:, c : c + P], words[:, u * P : (u + 1) * P], ident[:])
+
+        def CO(n):
+            copy(
+                n in ON_VECTOR["CO"],
+                fresh("og", n, [P, 1024], BF16)[:].bitcast(F32).rearrange("p (r c) -> p r c", c=4),
+                held["ot", n][:].rearrange("p (c r) -> p r c", c=4),
+            )
+
+        def QO(n):
+            s, g = divmod(n, 2)
+            cols = slice(256 * s, 256 * (s + 1))
+            nc.vector.quantize_mx(
+                out=out_c[:, g, cols].bitcast(FP8X4), scales=out_s[:, g, cols], in_=held["og", n][:]
+            )
+
+        def STW(lo, hi):
+            nc.sync.dma_start(
+                out=out_words[:, :, 1024 * lo : 1024 * hi].bitcast(I32),
+                in_=out_c[:, :, 256 * lo : 256 * hi].bitcast(I32),
+            )
+
+        def STS(lo, hi):
+            for q in range(4):
+                nc.sync.dma_start(
+                    out=out_2[:, 4 * q : 4 * q + 4, 256 * lo : 256 * hi].rearrange("g r m -> r g m").bitcast(I32),
+                    in_=out_s[32 * q : 32 * q + 4, :, 256 * lo : 256 * hi].bitcast(I32),
+                )
+
+        steps = dict(
+            MS=MS, GI=GI, LX0=LX0, LY0=LY0, LEW=LEW, LES=LES, LA=LA, MA=MA, GA=GA, GO=GO, GW=GW, W=W, TX0=TX0, CX0=CX0, QX0=QX0,
+            ME=ME, SE=SE, QE=QE, MAX=MAX, NEG=NEG, EXP=EXP, SUM=SUM, REC=REC, DIF=DIF, STT=STT, TX=TX, CX=CX,
+            QX=QX, TW=TW, CW=CW, QW=QW, MX=MX, SUB=SUB, CAST=CAST, STO=STO, TO=TO, CO=CO, QO=QO, STW=STW, STS=STS,
+            LOAD=load,
+        )
+        for name, *args in ORDER:
+            steps[name](*args)

@@ -23,64 +23,64 @@ PAIRS = TILES // 2
 
 LOAD_GROUPS = {'l': [(0, 1), (1, 2), (2, 4), (4, 8)], 'x': [(0, 1), (1, 2), (2, 4), (4, 6), (6, 8)], 'y': [(0, 1), (1, 2), (2, 4), (4, 6), (6, 8)]}
 BUFS = {'tp': 4, 'acc': 3, 'pq': 3, 'd': 2, 'w': 2, 'xg': 3, 'wg': 3, 'o': 6, 'ob': 6, 'og': 3, 'xc': 3, 'xs': 3, 'wc': 3, 'ws': 3}
-ON_VECTOR = {'CX0': [0], 'CX': [], 'CW': [12], 'CO': [13], 'CAST': [(14, 0), (15, 0)]}
-ON_GPSIMD = {'DIF': [1, 2, 3, 4, 5, 6, 7, 8, 9, 10, 11, 12, 13, 14, 15], 'CAST': [(1, 0), (0, 1), (2, 0), (3, 0), (4, 0), (5, 0), (6, 0), (6, 1), (8, 0), (10, 0), (11, 0), (12, 1), (13, 1), (15, 1)]}
+ON_VECTOR = {'CX0': [0], 'CX': [], 'CW': [14], 'CO': [12], 'CAST': [(13, 0), (15, 0)]}
+ON_GPSIMD = {'DIF': [0, 1, 2, 3, 4, 5, 6, 7, 8, 9, 10, 11, 12, 14, 13, 15], 'CAST': [(1, 1), (4, 0), (11, 1), (12, 1), (14, 1)]}
 ORDER = [
-    ('GA',), ('MS',), ('GW',), ('GO',), ('LOAD', 'l', 0), ('LX0', 0), ('LX0', 2), ('LOAD', 'l', 1),
-    ('LX0', 3), ('LA',), ('LOAD', 'l', 2), ('LX0', 1), ('LOAD', 'x', 0), ('LES',), ('LEW',), ('LY0', 0),
-    ('W', 0), ('GI',), ('W', 1), ('LOAD', 'x', 1), ('LY0', 1), ('W', 2), ('TX0', 0), ('W', 3),
-    ('MAX', 0), ('TX0', 2), ('MAX', 1), ('W', 4), ('W', 5), ('W', 6), ('TX0', 3), ('NEG', 0),
-    ('TX0', 1), ('LOAD', 'x', 2), ('MAX', 2), ('EXP', 0), ('NEG', 1), ('W', 7), ('SUM', 0), ('MAX', 3),
-    ('REC', 0), ('MA',), ('EXP', 1), ('NEG', 2), ('DIF', 0), ('CX0', 0), ('CX0', 3), ('SUM', 1),
-    ('MAX', 4), ('CX0', 2), ('REC', 1), ('TX', 1), ('EXP', 2), ('LOAD', 'l', 3), ('LOAD', 'y', 0), ('NEG', 3),
-    ('CX0', 1), ('DIF', 1), ('SUM', 2), ('MAX', 5), ('QX0', 1), ('STT', 0), ('QX0', 0), ('CX', 1),
-    ('REC', 2), ('TX', 0), ('TW', 0), ('STT', 1), ('EXP', 3), ('NEG', 4), ('CW', 0), ('ME', 3),
-    ('ME', 0), ('DIF', 2), ('SUM', 3), ('MAX', 6), ('QW', 0), ('REC', 3), ('TW', 1), ('ME', 1),
-    ('SE', 3), ('SE', 0), ('ME', 2), ('STT', 2), ('QX', 1), ('EXP', 4), ('NEG', 5), ('ME', 4),
-    ('CW', 1), ('LOAD', 'y', 2), ('LOAD', 'y', 1), ('CX', 0), ('QW', 1), ('LOAD', 'x', 3), ('SE', 1), ('SE', 2),
-    ('TX', 2), ('SE', 4), ('ME', 7), ('ME', 5), ('DIF', 3), ('QE', 0), ('SE', 7), ('QX', 0),
-    ('CX', 2), ('ME', 6), ('TX', 3), ('SE', 5), ('SUM', 4), ('MAX', 7), ('SE', 6), ('CX', 3),
-    ('REC', 4), ('QE', 1), ('TW', 2), ('TX', 4), ('STT', 3), ('QX', 2), ('MX', 0, 0), ('EXP', 5),
-    ('NEG', 6), ('CW', 2), ('MX', 1, 0), ('MX', 1, 1), ('QW', 2), ('SUB', 0, 0), ('DIF', 4), ('SUB', 1, 0),
-    ('SUM', 5), ('MAX', 8), ('CX', 4), ('REC', 5), ('SUB', 1, 1), ('TW', 3), ('TX', 5), ('STT', 4),
-    ('MX', 0, 1), ('QX', 3), ('EXP', 6), ('NEG', 7), ('CW', 3), ('MX', 2, 0), ('MX', 2, 1), ('QW', 3),
-    ('DIF', 5), ('SUB', 0, 1), ('SUB', 2, 0), ('SUM', 6), ('MAX', 9), ('CAST', 1, 0), ('CAST', 0, 0), ('CX', 5),
-    ('REC', 6), ('SUB', 2, 1), ('TW', 4), ('TO', 0), ('TX', 6), ('STT', 5), ('QX', 4), ('EXP', 7),
-    ('NEG', 8), ('CW', 4), ('MX', 3, 0), ('MX', 3, 1), ('QW', 4), ('DIF', 6), ('CAST', 0, 1), ('CAST', 1, 1),
-    ('SUB', 3, 0), ('SUM', 7), ('MAX', 10), ('CAST', 2, 0), ('CX', 6), ('REC', 7), ('SUB', 3, 1), ('TW', 5),
-    ('TX', 7), ('STT', 6), ('QX', 5), ('EXP', 8), ('NEG', 9), ('CW', 5), ('MX', 4, 0), ('MX', 4, 1),
-    ('QW', 5), ('DIF', 7), ('CO', 0), ('CAST', 2, 1), ('TO', 1), ('SUB', 4, 0), ('SUM', 8), ('MAX', 11),
-    ('CAST', 3, 0), ('CX', 7), ('REC', 8), ('SUB', 4, 1), ('TW', 6), ('TX', 8), ('STT', 7), ('QO', 0),
-    ('QX', 6), ('EXP', 9), ('NEG', 10), ('CW', 6), ('MX', 5, 0), ('MX', 5, 1), ('QW', 6), ('STO', 0),
-    ('DIF', 8), ('CO', 1), ('CAST', 3, 1), ('SUB', 5, 0), ('SUM', 9), ('MAX', 12), ('CAST', 4, 0), ('CX', 8),
-    ('REC', 9), ('SUB', 5, 1), ('TW', 7), ('TO', 2), ('TX', 9), ('STT', 8), ('QO', 1), ('QX', 7),
-    ('EXP', 10), ('NEG', 11), ('CW', 7), ('MX', 6, 0), ('MX', 6, 1), ('LOAD', 'x', 4), ('QW', 7), ('STO', 1),
-    ('DIF', 9), ('CO', 2), ('CAST', 4, 1), ('SUB', 6, 0), ('SUM', 10), ('MAX', 13), ('CAST', 5, 0), ('CX', 9),
-    ('REC', 10), ('SUB', 6, 1), ('TW', 8), ('TO', 3), ('TX', 10), ('STT', 9), ('QO', 2), ('QX', 8),
-    ('EXP', 11), ('NEG', 12), ('CW', 8), ('MX', 7, 0), ('MX', 7, 1), ('QW', 8), ('TX', 12), ('DIF', 10),
-    ('CO', 3), ('CAST', 5, 1), ('SUB', 7, 0), ('SUM', 11), ('MAX', 14), ('CAST', 6, 0), ('CX', 10), ('REC', 11),
-    ('SUB', 7, 1), ('TW', 9), ('TO', 4), ('TX', 11), ('STT', 10), ('QO', 3), ('QX', 9), ('LOAD', 'y', 3),
-    ('EXP', 12), ('NEG', 13), ('CW', 9), ('MX', 8, 0), ('MX', 8, 1), ('QW', 9), ('STO', 3), ('STO', 2),
-    ('DIF', 11), ('CO', 4), ('CAST', 6, 1), ('SUB', 8, 0), ('SUM', 12), ('MAX', 15), ('CX', 12), ('CAST', 7, 0),
-    ('CX', 11), ('REC', 12), ('SUB', 8, 1), ('TW', 10), ('TO', 5), ('STT', 11), ('QO', 4), ('QX', 10),
-    ('EXP', 13), ('NEG', 14), ('TX', 13), ('CW', 10), ('MX', 9, 0), ('MX', 9, 1), ('QW', 10), ('STO', 4),
-    ('DIF', 12), ('CO', 5), ('CAST', 7, 1), ('SUB', 9, 0), ('CAST', 8, 0), ('SUM', 13), ('REC', 13), ('SUB', 9, 1),
-    ('TW', 11), ('TO', 6), ('STT', 12), ('QO', 5), ('QX', 11), ('CX', 13), ('EXP', 14), ('NEG', 15),
-    ('CW', 11), ('MX', 10, 0), ('MX', 10, 1), ('QW', 11), ('STO', 5), ('DIF', 13), ('CO', 6), ('CAST', 8, 1),
-    ('SUB', 10, 0), ('SUM', 14), ('CAST', 9, 0), ('REC', 14), ('SUB', 10, 1), ('TW', 12), ('CW', 12), ('TO', 7),
-    ('TX', 14), ('QO', 6), ('QX', 12), ('EXP', 15), ('LOAD', 'y', 4), ('MX', 11, 0), ('MX', 11, 1), ('QW', 12),
-    ('STO', 6), ('DIF', 14), ('STT', 13), ('CO', 7), ('MX', 12, 0), ('CAST', 9, 1), ('SUB', 11, 0), ('SUM', 15),
-    ('CAST', 10, 0), ('CX', 14), ('REC', 15), ('STT', 14), ('SUB', 11, 1), ('TW', 13), ('TO', 8), ('TX', 15),
-    ('QO', 7), ('QX', 13), ('CW', 13), ('QW', 13), ('STO', 7), ('DIF', 15), ('CO', 8), ('CAST', 10, 1),
-    ('SUB', 12, 0), ('CAST', 11, 0), ('CX', 15), ('TW', 14), ('TO', 9), ('STT', 15), ('QO', 8), ('MX', 12, 1),
-    ('QX', 14), ('CW', 14), ('MX', 13, 0), ('MX', 13, 1), ('QW', 14), ('SUB', 12, 1), ('STO', 8), ('CO', 9),
-    ('CAST', 11, 1), ('SUB', 13, 0), ('CAST', 12, 0), ('SUB', 13, 1), ('TW', 15), ('TO', 10), ('QO', 9), ('QX', 15),
-    ('STW', 0, 2), ('CW', 15), ('MX', 14, 0), ('MX', 14, 1), ('QW', 15), ('STO', 9), ('CO', 10), ('CAST', 12, 1),
-    ('SUB', 14, 0), ('CAST', 13, 0), ('SUB', 14, 1), ('TO', 11), ('QO', 10), ('CAST', 14, 0), ('MX', 15, 0), ('MX', 15, 1),
-    ('STO', 10), ('CO', 11), ('CAST', 13, 1), ('TO', 12), ('QO', 11), ('STW', 2, 4), ('STO', 11), ('SUB', 15, 0),
-    ('CO', 12), ('CAST', 14, 1), ('SUB', 15, 1), ('CAST', 15, 0), ('TO', 13), ('QO', 12), ('STO', 12), ('CO', 13),
-    ('CAST', 15, 1), ('TO', 14), ('QO', 13), ('STO', 13), ('CO', 14), ('TO', 15), ('QO', 14), ('STO', 14),
-    ('CO', 15), ('STS', 0, 6), ('STW', 4, 6), ('QO', 15), ('STO', 15), ('STW', 6, 7), ('STS', 6, 8), ('STW', 7, 8),
+    ('GW',), ('MS',), ('GA',), ('GO',), ('LOAD', 'l', 0), ('LX0', 1), ('LOAD', 'l', 1), ('LX0', 0),
+    ('LA',), ('LX0', 3), ('LOAD', 'l', 2), ('LX0', 2), ('LOAD', 'x', 0), ('W', 0), ('LES',), ('LEW',),
+    ('LY0', 1), ('W', 1), ('LY0', 0), ('LOAD', 'l', 3), ('W', 2), ('W', 3), ('W', 4), ('LOAD', 'x', 1),
+    ('W', 5), ('LOAD', 'x', 2), ('W', 6), ('W', 7), ('LOAD', 'y', 0), ('MA',), ('LOAD', 'x', 4), ('LOAD', 'x', 3),
+    ('LOAD', 'y', 1), ('LOAD', 'y', 2), ('GI',), ('TX0', 1), ('TX0', 3), ('TX0', 0), ('TX0', 2), ('MAX', 0),
+    ('MAX', 1), ('NEG', 0), ('MAX', 2), ('NEG', 1), ('EXP', 0), ('SUM', 0), ('MAX', 3), ('DIF', 0),
+    ('EXP', 1), ('CX0', 1), ('CX0', 3), ('SUM', 1), ('MAX', 4), ('NEG', 3), ('NEG', 2), ('EXP', 2),
+    ('TX', 0), ('REC', 0), ('CX0', 2), ('MAX', 5), ('NEG', 4), ('EXP', 3), ('CX', 0), ('TX', 1),
+    ('STT', 0), ('CX0', 0), ('DIF', 1), ('REC', 1), ('QX0', 0), ('QX0', 1), ('SUM', 2), ('SUM', 3),
+    ('MAX', 6), ('NEG', 5), ('EXP', 4), ('ME', 4), ('ME', 7), ('STT', 1), ('REC', 2), ('REC', 3),
+    ('QX', 0), ('ME', 0), ('SUM', 4), ('MAX', 7), ('SE', 4), ('SE', 7), ('NEG', 6), ('TW', 0),
+    ('DIF', 2), ('EXP', 5), ('CW', 0), ('ME', 2), ('SE', 0), ('CX', 1), ('ME', 3), ('STT', 2),
+    ('DIF', 3), ('SE', 2), ('ME', 1), ('ME', 5), ('SUM', 5), ('SE', 3), ('SE', 1), ('MAX', 8),
+    ('NEG', 7), ('TW', 1), ('ME', 6), ('TX', 3), ('TW', 2), ('CW', 1), ('EXP', 6), ('TX', 2),
+    ('QE', 0), ('QX', 1), ('QW', 0), ('MX', 0, 0), ('TX', 4), ('QW', 1), ('STT', 3), ('DIF', 4),
+    ('REC', 4), ('CW', 2), ('SE', 6), ('CX', 2), ('SUM', 6), ('CX', 3), ('MAX', 9), ('NEG', 8),
+    ('SE', 5), ('TW', 3), ('EXP', 7), ('QX', 2), ('CX', 4), ('QE', 1), ('TX', 5), ('MX', 1, 0),
+    ('STT', 4), ('DIF', 5), ('REC', 5), ('QW', 2), ('SUB', 0, 0), ('CW', 3), ('MX', 0, 1), ('SUM', 7),
+    ('MAX', 10), ('NEG', 9), ('TW', 4), ('EXP', 8), ('SUB', 1, 0), ('CX', 5), ('TX', 6), ('QW', 3),
+    ('MX', 2, 0), ('STT', 5), ('DIF', 6), ('REC', 6), ('QX', 3), ('SUB', 0, 1), ('MX', 1, 1), ('CW', 4),
+    ('SUM', 8), ('MAX', 11), ('NEG', 10), ('TW', 5), ('EXP', 9), ('CAST', 0, 0), ('SUB', 2, 0), ('QX', 4),
+    ('CX', 6), ('SUB', 1, 1), ('TX', 7), ('QW', 4), ('STT', 6), ('DIF', 7), ('REC', 7), ('MX', 2, 1),
+    ('MX', 3, 0), ('MX', 3, 1), ('CW', 5), ('SUB', 2, 1), ('SUM', 9), ('NEG', 11), ('TW', 6), ('CAST', 0, 1),
+    ('CAST', 1, 0), ('EXP', 10), ('CAST', 1, 1), ('SUB', 3, 0), ('SUB', 3, 1), ('QX', 5), ('CX', 7), ('TX', 8),
+    ('QW', 5), ('MX', 4, 0), ('MAX', 12), ('STT', 7), ('DIF', 8), ('REC', 8), ('MX', 4, 1), ('TO', 1),
+    ('CW', 6), ('SUM', 10), ('MAX', 13), ('CAST', 3, 0), ('NEG', 12), ('TO', 0), ('TW', 7), ('EXP', 11),
+    ('SUB', 4, 0), ('SUB', 4, 1), ('QX', 6), ('CX', 8), ('TX', 9), ('QW', 6), ('MX', 5, 0), ('STT', 8),
+    ('DIF', 9), ('REC', 9), ('CO', 1), ('MX', 5, 1), ('CO', 0), ('CAST', 3, 1), ('CW', 7), ('SUM', 11),
+    ('MAX', 14), ('TW', 8), ('CAST', 2, 1), ('CAST', 2, 0), ('EXP', 12), ('SUB', 5, 0), ('SUB', 5, 1), ('QX', 7),
+    ('CX', 9), ('TX', 10), ('QW', 7), ('MX', 6, 0), ('STT', 9), ('DIF', 10), ('REC', 10), ('MX', 6, 1),
+    ('NEG', 13), ('LOAD', 'y', 3), ('CW', 8), ('LOAD', 'y', 4), ('STO', 0), ('SUM', 12), ('MAX', 15), ('NEG', 14),
+    ('TO', 2), ('TW', 9), ('CAST', 4, 0), ('EXP', 13), ('SUB', 6, 0), ('SUB', 6, 1), ('QX', 8), ('QO', 0),
+    ('CX', 10), ('TX', 11), ('QW', 8), ('MX', 7, 0), ('STT', 10), ('DIF', 11), ('REC', 11), ('MX', 7, 1),
+    ('CO', 2), ('CW', 9), ('STO', 1), ('TO', 3), ('TW', 10), ('CAST', 4, 1), ('CAST', 5, 0), ('QO', 1),
+    ('SUB', 7, 0), ('SUB', 7, 1), ('QX', 9), ('CX', 11), ('TX', 12), ('QW', 9), ('MX', 8, 0), ('STT', 11),
+    ('DIF', 12), ('REC', 12), ('MX', 8, 1), ('EXP', 14), ('CO', 3), ('CW', 10), ('STO', 2), ('SUM', 13),
+    ('SUM', 14), ('TO', 4), ('TW', 11), ('CAST', 5, 1), ('NEG', 15), ('CAST', 6, 0), ('QO', 2), ('SUB', 8, 0),
+    ('SUB', 8, 1), ('QX', 10), ('DIF', 14), ('CX', 12), ('TX', 13), ('QW', 10), ('MX', 9, 0), ('STT', 12),
+    ('DIF', 13), ('REC', 13), ('MX', 9, 1), ('CO', 4), ('CW', 11), ('STO', 3), ('TO', 5), ('TW', 12),
+    ('CAST', 6, 1), ('CAST', 7, 0), ('QO', 3), ('SUB', 9, 0), ('SUB', 9, 1), ('QX', 11), ('CX', 13), ('TX', 14),
+    ('QW', 11), ('MX', 10, 0), ('STT', 13), ('MX', 10, 1), ('CO', 5), ('CW', 12), ('STO', 4), ('TO', 6),
+    ('TW', 13), ('REC', 14), ('EXP', 15), ('CAST', 7, 1), ('CAST', 8, 0), ('QO', 4), ('SUB', 10, 0), ('SUM', 15),
+    ('SUB', 10, 1), ('QX', 12), ('CX', 14), ('TX', 15), ('QW', 12), ('MX', 11, 0), ('STT', 14), ('DIF', 15),
+    ('REC', 15), ('MX', 11, 1), ('CO', 6), ('CW', 13), ('STO', 5), ('TO', 7), ('TW', 14), ('CAST', 8, 1),
+    ('CAST', 9, 0), ('QO', 5), ('SUB', 11, 0), ('SUB', 11, 1), ('QX', 13), ('CX', 15), ('QW', 13), ('MX', 12, 0),
+    ('STT', 15), ('MX', 12, 1), ('CO', 7), ('MX', 13, 0), ('STW', 0, 2), ('CW', 14), ('STO', 6), ('TO', 8),
+    ('TW', 15), ('CAST', 9, 1), ('CAST', 10, 0), ('QO', 6), ('QW', 14), ('SUB', 12, 0), ('QX', 14), ('CO', 8),
+    ('CW', 15), ('STO', 7), ('TO', 9), ('MX', 13, 1), ('CAST', 10, 1), ('CAST', 11, 0), ('QO', 7), ('SUB', 12, 1),
+    ('SUB', 13, 0), ('SUB', 13, 1), ('QX', 15), ('QW', 15), ('MX', 14, 0), ('MX', 14, 1), ('CO', 9), ('STO', 8),
+    ('TO', 10), ('CAST', 11, 1), ('CAST', 12, 0), ('QO', 8), ('SUB', 14, 0), ('SUB', 14, 1), ('CO', 10), ('STO', 9),
+    ('TO', 11), ('CAST', 12, 1), ('CAST', 13, 0), ('QO', 9), ('CO', 11), ('MX', 15, 0), ('STO', 10), ('CAST', 13, 1),
+    ('CAST', 14, 0), ('QO', 10), ('MX', 15, 1), ('STO', 11), ('STW', 2, 4), ('TO', 13), ('TO', 12), ('QO', 11),
+    ('SUB', 15, 0), ('SUB', 15, 1), ('CO', 13), ('CAST', 15, 0), ('STO', 12), ('CAST', 14, 1), ('CO', 12), ('TO', 14),
+    ('CAST', 15, 1), ('QO', 12), ('CO', 14), ('STO', 13), ('TO', 15), ('QO', 13), ('CO', 15), ('STO', 14),
+    ('QO', 14), ('QO', 15), ('STW', 4, 6), ('STS', 0, 6), ('STO', 15), ('STW', 6, 7), ('STW', 7, 8), ('STS', 6, 8),
 ]
 
 

from contextlib import ExitStack

import concourse.mybir as mybir
from concourse.masks import make_identity

N, J, D, T = 2048, 512, 1024, 1024
FLOPS = 2 * N * D * T + 2 * J * D * T + 2 * N * J * T

F32 = mybir.dt.float32
BF16 = mybir.dt.bfloat16
I32 = mybir.dt.int32
U32 = mybir.dt.uint32
U8 = mybir.dt.uint8
FP8X4 = mybir.dt.float8_e4m3fn_x4
FP4X4 = mybir.dt.float4_e2m1fn_x4
ALU = mybir.AluOpType
ACT = mybir.ActivationFunctionType
AX = mybir.AxisListType

P = 128
TILES = N // P
PAIRS = TILES // 2

LOAD_GROUPS = {'l': [(0, 1), (1, 2), (2, 4), (4, 8)], 'x': [(0, 1), (1, 2), (2, 4), (4, 6), (6, 8)], 'y': [(0, 1), (1, 2), (2, 4), (4, 6), (6, 8)]}
BUFS = {'tp': 4, 'acc': 3, 'pq': 3, 'd': 2, 'w': 2, 'xg': 3, 'wg': 3, 'o': 6, 'ob': 6, 'og': 3, 'xc': 3, 'xs': 3, 'wc': 3, 'ws': 3}
ON_VECTOR = {'CX0': [0], 'CX': [], 'CW': [14], 'CO': [12], 'CAST': [(13, 0), (15, 0)]}
ON_GPSIMD = {'DIF': [0, 1, 2, 3, 4, 5, 6, 7, 8, 9, 10, 11, 12, 14, 13, 15], 'CAST': [(1, 1), (4, 0), (11, 1), (12, 1), (14, 1)]}
ORDER = [
    ('GW',), ('MS',), ('GA',), ('GO',), ('LOAD', 'l', 0), ('LX0', 1), ('LOAD', 'l', 1), ('LX0', 0),
    ('LA',), ('LX0', 3), ('LOAD', 'l', 2), ('LX0', 2), ('LOAD', 'x', 0), ('W', 0), ('LES',), ('LEW',),
    ('LY0', 1), ('W', 1), ('LY0', 0), ('LOAD', 'l', 3), ('W', 2), ('W', 3), ('W', 4), ('LOAD', 'x', 1),
    ('W', 5), ('LOAD', 'x', 2), ('W', 6), ('W', 7), ('LOAD', 'y', 0), ('MA',), ('LOAD', 'x', 4), ('LOAD', 'x', 3),
    ('LOAD', 'y', 1), ('LOAD', 'y', 2), ('GI',), ('TX0', 1), ('TX0', 3), ('TX0', 0), ('TX0', 2), ('MAX', 0),
    ('MAX', 1), ('NEG', 0), ('MAX', 2), ('NEG', 1), ('EXP', 0), ('SUM', 0), ('MAX', 3), ('DIF', 0),
    ('EXP', 1), ('CX0', 1), ('CX0', 3), ('SUM', 1), ('MAX', 4), ('NEG', 3), ('NEG', 2), ('EXP', 2),
    ('TX', 0), ('REC', 0), ('CX0', 2), ('MAX', 5), ('NEG', 4), ('EXP', 3), ('CX', 0), ('TX', 1),
    ('STT', 0), ('CX0', 0), ('DIF', 1), ('REC', 1), ('QX0', 0), ('QX0', 1), ('SUM', 2), ('SUM', 3),
    ('MAX', 6), ('NEG', 5), ('EXP', 4), ('ME', 4), ('ME', 7), ('STT', 1), ('REC', 2), ('REC', 3),
    ('QX', 0), ('ME', 0), ('SUM', 4), ('MAX', 7), ('SE', 4), ('SE', 7), ('NEG', 6), ('TW', 0),
    ('DIF', 2), ('EXP', 5), ('CW', 0), ('ME', 2), ('SE', 0), ('CX', 1), ('ME', 3), ('STT', 2),
    ('DIF', 3), ('SE', 2), ('ME', 1), ('ME', 5), ('SUM', 5), ('SE', 3), ('SE', 1), ('MAX', 8),
    ('NEG', 7), ('TW', 1), ('ME', 6), ('TX', 3), ('TW', 2), ('CW', 1), ('EXP', 6), ('TX', 2),
    ('QE', 0), ('QX', 1), ('QW', 0), ('MX', 0, 0), ('TX', 4), ('QW', 1), ('STT', 3), ('DIF', 4),
    ('REC', 4), ('CW', 2), ('SE', 6), ('CX', 2), ('SUM', 6), ('CX', 3), ('MAX', 9), ('NEG', 8),
    ('SE', 5), ('TW', 3), ('EXP', 7), ('QX', 2), ('CX', 4), ('QE', 1), ('TX', 5), ('MX', 1, 0),
    ('STT', 4), ('DIF', 5), ('REC', 5), ('QW', 2), ('SUB', 0, 0), ('CW', 3), ('MX', 0, 1), ('SUM', 7),
    ('MAX', 10), ('NEG', 9), ('TW', 4), ('EXP', 8), ('SUB', 1, 0), ('CX', 5), ('TX', 6), ('QW', 3),
    ('MX', 2, 0), ('STT', 5), ('DIF', 6), ('REC', 6), ('QX', 3), ('SUB', 0, 1), ('MX', 1, 1), ('CW', 4),
    ('SUM', 8), ('MAX', 11), ('NEG', 10), ('TW', 5), ('EXP', 9), ('CAST', 0, 0), ('SUB', 2, 0), ('QX', 4),
    ('CX', 6), ('SUB', 1, 1), ('TX', 7), ('QW', 4), ('STT', 6), ('DIF', 7), ('REC', 7), ('MX', 2, 1),
    ('MX', 3, 0), ('MX', 3, 1), ('CW', 5), ('SUB', 2, 1), ('SUM', 9), ('NEG', 11), ('TW', 6), ('CAST', 0, 1),
    ('CAST', 1, 0), ('EXP', 10), ('CAST', 1, 1), ('SUB', 3, 0), ('SUB', 3, 1), ('QX', 5), ('CX', 7), ('TX', 8),
    ('QW', 5), ('MX', 4, 0), ('MAX', 12), ('STT', 7), ('DIF', 8), ('REC', 8), ('MX', 4, 1), ('TO', 1),
    ('CW', 6), ('SUM', 10), ('MAX', 13), ('CAST', 3, 0), ('NEG', 12), ('TO', 0), ('TW', 7), ('EXP', 11),
    ('SUB', 4, 0), ('SUB', 4, 1), ('QX', 6), ('CX', 8), ('TX', 9), ('QW', 6), ('MX', 5, 0), ('STT', 8),
    ('DIF', 9), ('REC', 9), ('CO', 1), ('MX', 5, 1), ('CO', 0), ('CAST', 3, 1), ('CW', 7), ('SUM', 11),
    ('MAX', 14), ('TW', 8), ('CAST', 2, 1), ('CAST', 2, 0), ('EXP', 12), ('SUB', 5, 0), ('SUB', 5, 1), ('QX', 7),
    ('CX', 9), ('TX', 10), ('QW', 7), ('MX', 6, 0), ('STT', 9), ('DIF', 10), ('REC', 10), ('MX', 6, 1),
    ('NEG', 13), ('LOAD', 'y', 3), ('CW', 8), ('LOAD', 'y', 4), ('STO', 0), ('SUM', 12), ('MAX', 15), ('NEG', 14),
    ('TO', 2), ('TW', 9), ('CAST', 4, 0), ('EXP', 13), ('SUB', 6, 0), ('SUB', 6, 1), ('QX', 8), ('QO', 0),
    ('CX', 10), ('TX', 11), ('QW', 8), ('MX', 7, 0), ('STT', 10), ('DIF', 11), ('REC', 11), ('MX', 7, 1),
    ('CO', 2), ('CW', 9), ('STO', 1), ('TO', 3), ('TW', 10), ('CAST', 4, 1), ('CAST', 5, 0), ('QO', 1),
    ('SUB', 7, 0), ('SUB', 7, 1), ('QX', 9), ('CX', 11), ('TX', 12), ('QW', 9), ('MX', 8, 0), ('STT', 11),
    ('DIF', 12), ('REC', 12), ('MX', 8, 1), ('EXP', 14), ('CO', 3), ('CW', 10), ('STO', 2), ('SUM', 13),
    ('SUM', 14), ('TO', 4), ('TW', 11), ('CAST', 5, 1), ('NEG', 15), ('CAST', 6, 0), ('QO', 2), ('SUB', 8, 0),
    ('SUB', 8, 1), ('QX', 10), ('DIF', 14), ('CX', 12), ('TX', 13), ('QW', 10), ('MX', 9, 0), ('STT', 12),
    ('DIF', 13), ('REC', 13), ('MX', 9, 1), ('CO', 4), ('CW', 11), ('STO', 3), ('TO', 5), ('TW', 12),
    ('CAST', 6, 1), ('CAST', 7, 0), ('QO', 3), ('SUB', 9, 0), ('SUB', 9, 1), ('QX', 11), ('CX', 13), ('TX', 14),
    ('QW', 11), ('MX', 10, 0), ('STT', 13), ('MX', 10, 1), ('CO', 5), ('CW', 12), ('STO', 4), ('TO', 6),
    ('TW', 13), ('REC', 14), ('EXP', 15), ('CAST', 7, 1), ('CAST', 8, 0), ('QO', 4), ('SUB', 10, 0), ('SUM', 15),
    ('SUB', 10, 1), ('QX', 12), ('CX', 14), ('TX', 15), ('QW', 12), ('MX', 11, 0), ('STT', 14), ('DIF', 15),
    ('REC', 15), ('MX', 11, 1), ('CO', 6), ('CW', 13), ('STO', 5), ('TO', 7), ('TW', 14), ('CAST', 8, 1),
    ('CAST', 9, 0), ('QO', 5), ('SUB', 11, 0), ('SUB', 11, 1), ('QX', 13), ('CX', 15), ('QW', 13), ('MX', 12, 0),
    ('STT', 15), ('MX', 12, 1), ('CO', 7), ('MX', 13, 0), ('STW', 0, 2), ('CW', 14), ('STO', 6), ('TO', 8),
    ('TW', 15), ('CAST', 9, 1), ('CAST', 10, 0), ('QO', 6), ('QW', 14), ('SUB', 12, 0), ('QX', 14), ('CO', 8),
    ('CW', 15), ('STO', 7), ('TO', 9), ('MX', 13, 1), ('CAST', 10, 1), ('CAST', 11, 0), ('QO', 7), ('SUB', 12, 1),
    ('SUB', 13, 0), ('SUB', 13, 1), ('QX', 15), ('QW', 15), ('MX', 14, 0), ('MX', 14, 1), ('CO', 9), ('STO', 8),
    ('TO', 10), ('CAST', 11, 1), ('CAST', 12, 0), ('QO', 8), ('SUB', 14, 0), ('SUB', 14, 1), ('CO', 10), ('STO', 9),
    ('TO', 11), ('CAST', 12, 1), ('CAST', 13, 0), ('QO', 9), ('CO', 11), ('MX', 15, 0), ('STO', 10), ('CAST', 13, 1),
    ('CAST', 14, 0), ('QO', 10), ('MX', 15, 1), ('STO', 11), ('STW', 2, 4), ('TO', 13), ('TO', 12), ('QO', 11),
    ('SUB', 15, 0), ('SUB', 15, 1), ('CO', 13), ('CAST', 15, 0), ('STO', 12), ('CAST', 14, 1), ('CO', 12), ('TO', 14),
    ('CAST', 15, 1), ('QO', 12), ('CO', 14), ('STO', 13), ('TO', 15), ('QO', 13), ('CO', 15), ('STO', 14),
    ('QO', 14), ('QO', 15), ('STW', 4, 6), ('STS', 0, 6), ('STO', 15), ('STW', 6, 7), ('STW', 7, 8), ('STS', 6, 8),
]


def group_of(kind, pair):
    return [j for j, (lo, hi) in enumerate(LOAD_GROUPS[kind]) if lo <= pair < hi][0]


def tile_augmentedl1ballsyntheticcontrolgap_x2_kernel(
    tc, y1, x1, y0, x0, eta_words, eta_scales, l, a, out_0, out_1, out_2
):
    nc = tc.nc
    with ExitStack() as ctx:
        keep = ctx.enter_context(tc.tile_pool(name="keep", bufs=1))
        work = ctx.enter_context(tc.tile_pool(name="work", bufs=2))
        stat = ctx.enter_context(tc.tile_pool(name="stat", bufs=TILES))
        psum = ctx.enter_context(tc.psum_pool(name="psum", bufs=1))
        ctx.enter_context(tc.manual_schedule())

        ident = keep.tile([P, P], F32, name="ident")
        ones = keep.tile([P, P], BF16, name="ones")
        a_row = keep.tile([P, J], BF16, name="a_row")
        gain = psum.tile([P, J], F32, name="gain")
        idle = keep.tile([P, J], BF16, name="idle")
        eta_w = keep.tile([P, 2, 2 * T], U8, name="eta_w", align_bytes=64)
        eta_s = keep.tile([P, 2, T], U8, name="eta_s", align_bytes=64)
        x0_sb = keep.tile([P, 4, D], BF16, name="x0_sb")
        y0_sb = keep.tile([P, 2, 4, 512], BF16, name="y0_sb")
        x0_g = keep.tile([P, 4, D], BF16, name="x0_g", align_bytes=64)
        x0_c = keep.tile([P, 4, 2, P], U32, name="x0_c", align_bytes=64)
        x0_s = keep.tile([P, 4, 2, P], U8, name="x0_s", align_bytes=64)
        e0_g = keep.tile([P, T, 4], BF16, name="e0_g", align_bytes=64)
        e0_c = keep.tile([P, T], U32, name="e0_c", align_bytes=64)
        e0_s = keep.tile([P, T], U8, name="e0_s", align_bytes=64)
        out_c = keep.tile([P, 2, N], U32, name="out_c", align_bytes=64)
        out_s = keep.tile([P, 2, N], U8, name="out_s", align_bytes=64)

        sources = {
            "l": l.rearrange("(s p i) k -> p s (i k)", p=P, i=2),
            "x": x1.rearrange("(s p i) k -> p s (i k)", p=P, i=2),
            "y": y1.rearrange("(s p i) k -> p s (i k)", p=P, i=2),
        }
        out_rows = out_0.rearrange("(s p i) k -> s i p k", p=P, i=2)
        out_words = out_1.rearrange("g p m t -> p g (m t)")
        held = {}

        def bank(tag, key):
            held[key] = psum.tile([P, 512], F32, name=tag, bufs=BUFS[tag])
            return held[key]

        def fresh(tag, n, shape, dtype):
            held[tag, n] = work.tile(shape, dtype, name=tag, bufs=BUFS[tag], align_bytes=64)
            return held[tag, n]

        def column(tag, n, width=1):
            held[tag, n] = stat.tile([P, width], F32, name=tag)
            return held[tag, n]

        def rows(kind, n):
            j = group_of(kind, n // 2)
            width = sources[kind].shape[2] // 2
            return held[kind, j][:, n // 2 - LOAD_GROUPS[kind][j][0], (n % 2) * width : (n % 2 + 1) * width]

        def load(kind, j):
            lo, hi = LOAD_GROUPS[kind][j]
            held[kind, j] = keep.tile([P, hi - lo, sources[kind].shape[2]], BF16, name="%s_in%d" % (kind, j))
            nc.sync.dma_start(out=held[kind, j][:], in_=sources[kind][:, lo:hi, :])

        def copy(on_vector, out, in_):
            if on_vector:
                nc.vector.tensor_copy(out=out, in_=in_)
            else:
                nc.scalar.copy(out=out, in_=in_)

        def transpose_k_last(src, dst):
            words = src.bitcast(F32)
            for g in range(2):
                for u in range(2):
                    c = (2 * g + u) * P
                    nc.tensor.transpose(dst[:, c : c + P], words[:, 256 * g + u : 256 * (g + 1) : 2], ident[:])

        def gather_k_last(on_vector, src, dst):
            copy(
                on_vector,
                dst.bitcast(F32).rearrange("p (g r u) -> p g r u", g=2, u=2),
                src[:].rearrange("p (g u r) -> p g r u", g=2, u=2),
            )

        def MS():
            nc.vector.memset(eta_s[:].rearrange("p g n -> p (g n)").bitcast(I32), 0)

        def GI():
            make_identity(nc, ident[:])

        def GA():
            nc.vector.memset(a_row[:], 0.0)

        def GO():
            nc.vector.memset(ones[:], 1.0)

        def GW():
            nc.vector.memset(idle[:], 0.0)

        def W(j):
            nc.tensor.matmul(gain[:], lhsT=ones[:], rhs=idle[:], start=True, stop=True)

        def LX0(t):
            nc.sync.dma_start(out=x0_sb[:, t, :], in_=x0.rearrange("(p t) k -> p t k", t=4)[:, t, :])

        def LY0(h):
            cols = slice(512 * h, 512 * (h + 1))
            nc.sync.dma_start(out=y0_sb[:, h], in_=y0.rearrange("(p t) k -> p t k", t=4)[:, :, cols])

        def LEW():
            nc.sync.dma_start(out=eta_w[:].bitcast(I32), in_=eta_words.rearrange("g p b -> p g b").bitcast(I32))

        def LES():
            for q in range(4):
                nc.sync.dma_start(
                    out=eta_s[32 * q : 32 * q + 4, :, :].bitcast(I32),
                    in_=eta_scales[:, 4 * q : 4 * q + 4, :].rearrange("g r n -> r g n").bitcast(I32),
                )

        def LA():
            nc.sync.dma_start(out=a_row[0:1, :], in_=a.rearrange("(o n) -> o n", o=1))

        def MA():
            nc.tensor.matmul(
                gain[:], lhsT=ones[:], rhs=a_row[:].rearrange("p (q u e) -> p u q e", u=2, e=2), start=True, stop=True
            )

        def TX0(t):
            transpose_k_last(x0_sb[:, t, :], bank("tp", ("x0", t)))

        def CX0(t):
            gather_k_last(t in ON_VECTOR["CX0"], held["x0", t], x0_g[:, t, :])

        def QX0(h):
            nc.vector.quantize_mx(
                out=x0_c[:, 2 * h : 2 * h + 2].rearrange("p t g r -> p (t g r)").bitcast(FP8X4),
                scales=x0_s[:, 2 * h : 2 * h + 2].rearrange("p t g r -> p (t g r)"),
                in_=x0_g[:, 2 * h : 2 * h + 2, :].rearrange("p t k -> p (t k)"),
            )

        def ME(c):
            acc = bank("acc", ("e", c))
            for t in range(4):
                for g in range(2):
                    nc.tensor.matmul_mx(
                        out=acc[:, t * P : (t + 1) * P],
                        lhsT=x0_c[:, t, g, :].bitcast(FP8X4),
                        lhsT_scale=x0_s[:, t, g, :],
                        rhs=eta_w[:, g, 2 * P * c : 2 * P * (c + 1)].bitcast(FP4X4),
                        rhs_scale=eta_s[:, g, P * c : P * (c + 1)],
                        start=(g == 0),
                        stop=(g == 1),
                    )

        def SE(c):
            nc.vector.tensor_tensor(
                out=e0_g[:, P * c : P * (c + 1), :],
                in0=y0_sb[:, c // 4, :, P * (c % 4) : P * (c % 4 + 1)].rearrange("p t n -> p n t"),
                in1=held["e", c][:].rearrange("p (t n) -> p n t", t=4),
                op=ALU.subtract,
            )

        def QE(h):
            cols = slice(512 * h, 512 * (h + 1))
            nc.vector.quantize_mx(
                out=e0_c[:, cols].bitcast(FP8X4),
                scales=e0_s[:, cols],
                in_=e0_g[:, cols, :].rearrange("p n t -> p (n t)"),
            )

        def MAX(n):
            nc.vector.tensor_reduce(
                out=column("top", n)[:], in_=rows("l", n), axis=AX.X, op=ALU.max, apply_absolute_value=True
            )

        def NEG(n):
            nc.gpsimd.tensor_scalar(
                out=column("shift", n)[:], in0=held["top", n][:], scalar1=-1.0, scalar2=0.0, op0=ALU.mult, op1=ALU.add
            )

        def EXP(n):
            pq = fresh("pq", n, [P, 2, J], F32)
            sums = column("sums", n, 2)
            for side, sign in enumerate((1.0, -1.0)):
                nc.scalar.activation(
                    out=pq[:, side, :].rearrange("p (u q e) -> p u q e", u=2, e=2),
                    in_=rows("l", n).rearrange("p (q u e) -> p u q e", u=2, e=2),
                    func=ACT.Exp,
                    bias=held["shift", n][:],
                    scale=sign,
                    accum_out=sums[:, side : side + 1],
                )

        def SUM(n):
            sums = held["sums", n]
            nc.gpsimd.tensor_tensor(out=column("total", n)[:], in0=sums[:, 0:1], in1=sums[:, 1:2], op=ALU.add)

        def REC(n):
            nc.vector.reciprocal(out=column("recip", n)[:], in_=held["total", n][:])

        def DIF(n):
            engine = nc.gpsimd if n in ON_GPSIMD["DIF"] else nc.vector
            pq = held["pq", n]
            engine.tensor_tensor(out=fresh("d", n, [P, J], F32)[:], in0=pq[:, 0, :], in1=pq[:, 1, :], op=ALU.subtract)

        def STT(n):
            nc.vector.scalar_tensor_tensor(
                out=fresh("w", n, [P, J], BF16)[:],
                in0=held["d", n][:],
                scalar=held["recip", n][:],
                in1=gain[:],
                op0=ALU.mult,
                op1=ALU.mult,
            )

        def TX(n):
            transpose_k_last(rows("x", n), bank("tp", ("xt", n)))

        def CX(n):
            gather_k_last(n in ON_VECTOR["CX"], held["xt", n], fresh("xg", n, [P, D], BF16)[:])

        def QX(n):
            nc.vector.quantize_mx(
                out=fresh("xc", n, [P, 2 * P], U32)[:].bitcast(FP8X4),
                scales=fresh("xs", n, [P, 2 * P], U8)[:],
                in_=held["xg", n][:],
            )

        def TW(n):
            dst = bank("tp", ("wt", n))
            words = held["w", n][:].bitcast(F32)
            for u in range(2):
                nc.tensor.transpose(dst[:, u * P : (u + 1) * P], words[:, u * P : (u + 1) * P], ident[:])

        def CW(n):
            copy(
                n in ON_VECTOR["CW"],
                fresh("wg", n, [P, J], BF16)[:].bitcast(F32).rearrange("p (r u) -> p r u", u=2),
                held["wt", n][:, 0 : 2 * P].rearrange("p (u r) -> p r u", u=2),
            )

        def QW(n):
            nc.vector.quantize_mx(
                out=fresh("wc", n, [P, P], U32)[:].bitcast(FP8X4),
                scales=fresh("ws", n, [P, P], U8)[:],
                in_=held["wg", n][:],
            )

        def MX(n, h):
            acc = bank("acc", ("acc", n, h))
            for g in range(2):
                nc.tensor.matmul_mx(
                    out=acc[:],
                    lhsT=held["xc", n][:, g * P : (g + 1) * P].bitcast(FP8X4),
                    lhsT_scale=held["xs", n][:, g * P : (g + 1) * P],
                    rhs=eta_w[:, g, 1024 * h : 1024 * (h + 1)].bitcast(FP4X4),
                    rhs_scale=eta_s[:, g, 512 * h : 512 * (h + 1)],
                    start=(g == 0),
                    stop=False,
                )
            nc.tensor.matmul_mx(
                out=acc[:],
                lhsT=held["wc", n][:].bitcast(FP8X4),
                lhsT_scale=held["ws", n][:],
                rhs=e0_c[:, 512 * h : 512 * (h + 1)].bitcast(FP8X4),
                rhs_scale=e0_s[:, 512 * h : 512 * (h + 1)],
                start=False,
                stop=True,
            )

        def SUB(n, h):
            o = held["o", n] if h else fresh("o", n, [P, T], F32)
            cols = slice(512 * h, 512 * (h + 1))
            nc.vector.tensor_tensor(
                out=o[:, cols], in0=rows("y", n)[:, cols], in1=held["acc", n, h][:], op=ALU.subtract
            )

        def CAST(n, h):
            dst = fresh("ob", (n, h), [P, 512], BF16)[:].rearrange("p (u q e) -> p u q e", u=2, e=2)
            src = held["o", n][:, 512 * h : 512 * (h + 1)].rearrange("p (q u e) -> p u q e", u=2, e=2)
            if (n, h) in ON_GPSIMD["CAST"]:
                nc.gpsimd.tensor_scalar(out=dst, in0=src, scalar1=1.0, scalar2=1.0, op0=ALU.mult, op1=ALU.mult)
            else:
                copy((n, h) in ON_VECTOR["CAST"], dst, src)

        def STO(n):
            nc.sync.dma_start(out=out_rows[n // 2, n % 2], in_=held["o", n][:])

        def TO(n):
            s, g = divmod(n, 2)
            dst = bank("tp", ("ot", n))
            for i in range(2):
                words = held["ob", (2 * s + i, g)][:].bitcast(F32)
                for u in range(2):
                    c = (2 * i + u) * P
                    nc.tensor.transpose(dst[:, c : c + P], words[:, u * P : (u + 1) * P], ident[:])

        def CO(n):
            copy(
                n in ON_VECTOR["CO"],
                fresh("og", n, [P, 1024], BF16)[:].bitcast(F32).rearrange("p (r c) -> p r c", c=4),
                held["ot", n][:].rearrange("p (c r) -> p r c", c=4),
            )

        def QO(n):
            s, g = divmod(n, 2)
            cols = slice(256 * s, 256 * (s + 1))
            nc.vector.quantize_mx(
                out=out_c[:, g, cols].bitcast(FP8X4), scales=out_s[:, g, cols], in_=held["og", n][:]
            )

        def STW(lo, hi):
            nc.sync.dma_start(
                out=out_words[:, :, 1024 * lo : 1024 * hi].bitcast(I32),
                in_=out_c[:, :, 256 * lo : 256 * hi].bitcast(I32),
            )

        def STS(lo, hi):
            for q in range(4):
                nc.sync.dma_start(
                    out=out_2[:, 4 * q : 4 * q + 4, 256 * lo : 256 * hi].rearrange("g r m -> r g m").bitcast(I32),
                    in_=out_s[32 * q : 32 * q + 4, :, 256 * lo : 256 * hi].bitcast(I32),
                )

        steps = dict(
            MS=MS, GI=GI, LX0=LX0, LY0=LY0, LEW=LEW, LES=LES, LA=LA, MA=MA, GA=GA, GO=GO, GW=GW, W=W, TX0=TX0, CX0=CX0, QX0=QX0,
            ME=ME, SE=SE, QE=QE, MAX=MAX, NEG=NEG, EXP=EXP, SUM=SUM, REC=REC, DIF=DIF, STT=STT, TX=TX, CX=CX,
            QX=QX, TW=TW, CW=CW, QW=QW, MX=MX, SUB=SUB, CAST=CAST, STO=STO, TO=TO, CO=CO, QO=QO, STW=STW, STS=STS,
            LOAD=load,
        )
        for name, *args in ORDER:
            steps[name](*args)
